import numpy as np
import ml_dtypes


def mxq(x, axis, fmt="e4m3"):
    dtype, down = {"e4m3": (ml_dtypes.float8_e4m3fn, 7), "e5m2": (ml_dtypes.float8_e5m2, 14)}[fmt]
    v = np.moveaxis(np.asarray(x, np.float32).astype(ml_dtypes.bfloat16).astype(np.float64), axis, -1)
    blocks = v.reshape(v.shape[:-1] + (-1, 32))
    amax = np.abs(blocks).max(-1, keepdims=True)
    byte = np.maximum(np.where(amax > 0, np.frexp(amax)[1] - 1 + 127, 0) - down, 1)
    scale = np.exp2(byte - 127.0)
    codes = (blocks / scale).astype(np.float32).astype(dtype).astype(np.float64)
    return np.moveaxis((codes * scale).reshape(v.shape), -1, axis)


WIDE = False


def mx_kscale(k):
    if not WIDE:
        return np.ones(k)
    levels = np.array([10, -10, 5, -5, 0])
    if k % 512:
        return np.exp2(np.random.permutation(np.resize(levels, k // 32))).repeat(32)
    a = np.empty((k // 512, 16))
    for p in range(k // 512):
        a[p, :8] = np.random.permutation(np.resize(levels, 8))
        for g in range(8):
            far = levels[np.abs(levels - a[p, g]) >= 10]
            a[p, g + 8] = far[np.random.randint(len(far))]
    return np.exp2(a.ravel()).repeat(32)


BF16 = ml_dtypes.bfloat16


def bf(x):
    return np.asarray(x, np.float32).astype(BF16)


def f64(x):
    return np.asarray(x).astype(np.float64)


N, D, K, V = 4096, 512, 2, 512


def log_sum_exp(x, axis):
    m = np.max(x, axis=axis, keepdims=True)
    return m + np.log(np.sum(np.exp(x - m), axis=axis, keepdims=True))


def log_normalize(x, axis):
    s = x - np.max(x, axis=axis, keepdims=True)
    return s - np.log(np.sum(np.exp(s), axis=axis, keepdims=True))


def draw0():
    s = mx_kscale(D)
    t = mx_kscale(D)
    return {"h": bf(np.random.standard_normal((N, D)) * s),
            "w": bf(np.random.standard_normal((K, D, D)) / np.sqrt(D) / s[None, :, None]),
            "g": bf((1.0 + 0.1 * np.random.standard_normal((K, D))) * t),
            "u": bf(np.random.standard_normal((K, D)) * 2.0 / np.sqrt(D)),
            "emb": bf(np.random.standard_normal((V, D)) * 3.0 / np.sqrt(D) / t)}


def core(h, w, g, u, emb):
    n, d = h.shape
    k = w.shape[0]
    vocab = emb.shape[0]
    c = mxq(f64(h), 1, "e4m3") @ mxq(f64(w), 1, "e4m3")
    t = np.tanh(c.transpose(1, 0, 2))
    a = t * f64(g)[None, :, :]
    aq = mxq(a.reshape(n * k, d), 1, "e4m3")
    l = (aq @ mxq(f64(emb), 1, "e4m3").T).reshape(n, k, vocab)
    z = np.sum(t * f64(u)[None, :, :], axis=-1)
    logpi = log_normalize(z, axis=-1)
    lp = log_normalize(l, axis=-1)
    joint = logpi[:, :, None] + lp
    mixed = np.squeeze(log_sum_exp(joint, axis=1), axis=1)
    return mixed + np.log(vocab)


def e4m3fn_bytes(y):
    return np.clip(np.asarray(y, np.float64), -448.0, 448.0).astype(np.float32).astype(ml_dtypes.float8_e4m3fn).view(np.uint8)


def e4m3fn_values(b):
    return np.asarray(b, np.uint8).view(ml_dtypes.float8_e4m3fn).astype(np.float64)


def setup_inputs():
    d = draw0()
    x0 = np.asarray(d['h']).astype(np.float64)
    s = (np.max(np.abs(x0), axis=(0,), keepdims=True) / 448.0).astype(np.float32)
    out = {}
    for k, v in d.items():
        if k == 'h':
            out['h_bytes'] = e4m3fn_bytes(x0 / s.astype(np.float64))
            out['h_scale'] = s
        else:
            out[k] = v
    return out


def reference(h_bytes, h_scale, w, g, u, emb):
    return core(e4m3fn_values(h_bytes) * h_scale.astype(np.float64), w, g, u, emb)

from contextlib import ExitStack
import math

import concourse.mybir as mybir
from concourse.masks import make_identity

N, D, K, V = 4096, 512, 2, 512
P = 128
FLOPS = 2 * N * D * D * K + 2 * N * K * D * V + 2 * N * K * D

F32 = mybir.dt.float32
BF16 = mybir.dt.bfloat16
U32 = mybir.dt.uint32
U8 = mybir.dt.uint8
FP8 = mybir.dt.float8_e4m3fn
FP8X4 = mybir.dt.float8_e4m3fn_x4
ALU = mybir.AluOpType
ACT = mybir.ActivationFunctionType

ROWS = 512
GROUPS = N // ROWS
TPG = ROWS // P
TILES = N // P
BATCH_ENDS = (10, 20, 28, 32)
LIVE = 14
RATIO_CAP = float(2 ** 40)


def tile_mixtureofsoftmaxeshead_t_kernel(tc, h_bytes, h_scale, w, g, u, emb, out):
    nc = tc.nc
    with ExitStack() as ctx:
        keep = ctx.enter_context(tc.tile_pool(name="keep", bufs=1))
        work = ctx.enter_context(tc.tile_pool(name="work", bufs=2))
        psum = ctx.enter_context(tc.psum_pool(name="psum", bufs=1))
        ctx.enter_context(tc.manual_schedule())

        byts, hbf, trp, hb, hq, hs_q = {}, {}, {}, {}, {}, {}
        t_sb, a_bf, aq, as_ = {}, {}, {}, {}
        zps = {}
        cps = {}
        lps, dps = {}, {}
        nl0, l1, e_t = {}, {}, {}
        bias_t, ratio_t, stat_t = {}, {}, {}

        nm = keep.tile([P, K, TILES], F32, name="nm")
        ssum = keep.tile([P, K, TILES], F32, name="ssum")
        zz = keep.tile([P, K, TILES], F32, name="zz")
        dz = keep.tile([P, TILES], F32, name="dz")
        dlt = keep.tile([P, TILES], F32, name="dlt")
        m1 = keep.tile([P, TILES], F32, name="m1")

        warm = keep.tile([P, 1], F32, name="warm")
        warm2 = keep.tile([P, 1], F32, name="warm2")
        nc.vector.memset(warm[:], 0.0)
        nc.scalar.activation(out=warm2[:], in_=warm[:], func=ACT.Exp)

        ident = keep.tile([P, P], F32, name="ident")
        make_identity(nc, ident[:])

        def load(gi):
            t = work.tile([P, TPG * D], U8, name="byts", bufs=3, align_bytes=64)
            byts[gi] = t
            nc.sync.dma_start(
                out=t[:],
                in_=h_bytes[gi * ROWS:(gi + 1) * ROWS, :].rearrange("(r b) k -> r (b k)", b=TPG),
            )

        load(0)
        hsc = keep.tile([P, 4], F32, name="hsc")
        nc.sync.dma_start(out=hsc[:], in_=h_scale.rearrange("o (p t) -> p (o t)", t=4))
        w_raw = []
        for k in range(K):
            wr = keep.tile([P, 4, D], BF16, name="w_raw%d" % k)
            nc.sync.dma_start(out=wr[:], in_=w[k].rearrange("(p j) c -> p j c", j=4))
            w_raw.append(wr)
        g_raw = keep.tile([P, K, 4], BF16, name="g_raw")
        nc.sync.dma_start(out=g_raw[:], in_=g.rearrange("k (p s) -> p k s", s=4))
        u_raw = keep.tile([P, K, 4], BF16, name="u_raw")
        nc.sync.dma_start(out=u_raw[:], in_=u.rearrange("k (p s) -> p k s", s=4))
        load(1)
        emb_sb = keep.tile([P, 4, D], BF16, name="emb_sb")
        nc.sync.dma_start(out=emb_sb[:], in_=emb.rearrange("(b r) e -> r b e", b=4))

        g_sb = keep.tile([P, K, 4], F32, name="g_sb")
        u_sb = keep.tile([P, K, 4], F32, name="u_sb")
        wq = [keep.tile([P, D], U32, name="wq%d" % k, align_bytes=64) for k in range(K)]
        ws = [keep.tile([P, D], U8, name="ws%d" % k, align_bytes=64) for k in range(K)]
        eq = keep.tile([P, V], U32, name="eq", align_bytes=64)
        es = keep.tile([P, V], U8, name="es", align_bytes=64)
        neq = keep.tile([P, V], U32, name="neq", align_bytes=64)
        nes = keep.tile([P, V], U8, name="nes", align_bytes=64)

        def widen(gi):
            t = work.tile([P, TPG, D], BF16, name="hbf", bufs=2, align_bytes=64)
            hbf[gi] = t
            flat = t[:].rearrange("p b k -> p (b k)")
            if gi == 0:
                nc.vector.tensor_copy(out=flat, in_=byts[gi][:].bitcast(FP8))
            else:
                nc.gpsimd.tensor_copy(out=flat, in_=byts[gi][:].bitcast(FP8))

        def transposes(dst, src_words, half):
            for b in (2 * half, 2 * half + 1):
                for uu in (0, 1):
                    nc.tensor.transpose(
                        dst[:, uu, P * (b % 2):P * (b % 2) + P],
                        src_words[:, b, uu:D // 2:2],
                        ident[:],
                    )

        def h_transpose(gi, half):
            pt = psum.tile([P, 2, 256], F32, name="trp", tag="tr", bufs=1)
            trp[gi, half] = pt
            transposes(pt, hbf[gi][:].bitcast(F32), half)

        def h_scale_mul(gi, half):
            if half == 0:
                hb[gi] = work.tile([P, ROWS, 4], BF16, name="hb", bufs=2, align_bytes=64)
            nc.vector.tensor_tensor(
                out=hb[gi][:, half * 256:(half + 1) * 256, :].rearrange("p n (u e) -> p n u e", e=2),
                in0=trp[gi, half][:].bitcast(BF16).rearrange("p u (n e) -> p n u e", e=2),
                in1=hsc[:].rearrange("p (u e) -> p u e", e=2).unsqueeze(1).to_broadcast([P, 256, 2, 2]),
                op=ALU.mult,
            )

        def h_quant(gi):
            q = work.tile([P, ROWS], U32, name="hq", bufs=2, align_bytes=64)
            sc = work.tile([P, ROWS], U8, name="hqs", bufs=2, align_bytes=64)
            hq[gi], hs_q[gi] = q, sc
            nc.vector.quantize_mx(out=q[:].bitcast(FP8X4), scales=sc[:], in_=hb[gi][:].rearrange("p n t -> p (n t)"))

        def c_mm(gi, k, s):
            ps = psum.tile([P, ROWS], F32, name="cps", tag="c", bufs=3)
            cps[gi, k, s] = ps
            nc.tensor.matmul_mx(
                out=ps[:],
                lhsT=wq[k][:, s * P:(s + 1) * P].bitcast(FP8X4), lhsT_scale=ws[k][:, s * P:(s + 1) * P],
                rhs=hq[gi][:].bitcast(FP8X4), rhs_scale=hs_q[gi][:],
                start=True, stop=True,
            )

        def tanh(gi, k, s):
            if s == 0:
                t_sb[gi, k] = work.tile([P, 4, ROWS], F32, name="t_sb", bufs=4, align_bytes=64)
            nc.scalar.activation(out=t_sb[gi, k][:, s, :], in_=cps[gi, k, s][:], func=ACT.Tanh)

        def gain(gi, k):
            a = work.tile([P, ROWS, 4], BF16, name="a_bf", bufs=3, align_bytes=64)
            a_bf[gi, k] = a
            eng = nc.vector if k == 0 or gi == 0 else nc.gpsimd
            eng.tensor_tensor(
                out=a[:],
                in0=t_sb[gi, k][:].rearrange("p s n -> p n s"),
                in1=g_sb[:, k, :].unsqueeze(1).to_broadcast([P, ROWS, 4]),
                op=ALU.mult,
            )

        def a_quant(gi, k):
            q = work.tile([P, ROWS], U32, name="aq", bufs=6, align_bytes=64)
            sc = work.tile([P, ROWS], U8, name="aqs", bufs=6, align_bytes=64)
            aq[gi, k], as_[gi, k] = q, sc
            nc.vector.quantize_mx(out=q[:].bitcast(FP8X4), scales=sc[:], in_=a_bf[gi, k][:].rearrange("p n s -> p (n s)"))

        def z_mm(gi, k, j):
            if (k, j) == (0, 0):
                zps[gi] = psum.tile([P, K, TPG], F32, name="zps", tag="z", bufs=1)
            for s in range(4):
                nc.tensor.matmul(
                    out=zps[gi][:, k, j:j + 1],
                    lhsT=t_sb[gi, k][:, s, j * P:(j + 1) * P],
                    rhs=u_sb[:, k, s:s + 1],
                    start=(s == 0), stop=(s == 3),
                )

        def z_out(gi):
            cols = slice(gi * TPG, (gi + 1) * TPG)
            nc.vector.tensor_copy(out=zz[:, :, cols], in_=zps[gi][:])
            nc.vector.tensor_sub(out=dz[:, cols], in0=zz[:, 1, cols], in1=zz[:, 0, cols])

        def a_cols(gi, k, j):
            return aq[gi, k][:, j * P:(j + 1) * P].bitcast(FP8X4), as_[gi, k][:, j * P:(j + 1) * P]

        def l_mm(i):
            gi, j = divmod(i, TPG)
            for k in range(K):
                ps = psum.tile([P, V], F32, name="lps", tag="l", bufs=2)
                lps[i, k] = ps
                q, sc = a_cols(gi, k, j)
                nc.tensor.matmul_mx(out=ps[:], lhsT=q, lhsT_scale=sc, rhs=eq[:].bitcast(FP8X4), rhs_scale=es[:],
                                    start=True, stop=True)

        def d_mm(i):
            gi, j = divmod(i, TPG)
            ps = psum.tile([P, V], F32, name="dps", tag="d", bufs=1)
            dps[i] = ps
            q, sc = a_cols(gi, 1, j)
            nc.tensor.matmul_mx(out=ps[:], lhsT=q, lhsT_scale=sc, rhs=eq[:].bitcast(FP8X4), rhs_scale=es[:],
                                start=True, stop=False)
            q, sc = a_cols(gi, 0, j)
            nc.tensor.matmul_mx(out=ps[:], lhsT=q, lhsT_scale=sc, rhs=neq[:].bitcast(FP8X4), rhs_scale=nes[:],
                                start=False, stop=True)

        def copymax0(i):
            nl0[i] = work.tile([P, V], F32, name="nl0", bufs=LIVE)
            nc.vector.tensor_scalar(out=nl0[i][:], in0=lps[i, 0][:], scalar1=-1.0, scalar2=None,
                                    op0=ALU.mult, op1=ALU.min, accum_out=nm[:, 0, i:i + 1])

        def copymax1(i):
            l1[i] = work.tile([P, V], F32, name="l1", bufs=LIVE)
            nc.vector.tensor_scalar(out=l1[i][:], in0=lps[i, 1][:], scalar1=1.0, scalar2=None,
                                    op0=ALU.mult, op1=ALU.max, accum_out=m1[:, i:i + 1])

        def row_shift(i):
            nc.vector.tensor_scalar(out=nm[:, 1, i:i + 1], in0=m1[:, i:i + 1], scalar1=-1.0, scalar2=None, op0=ALU.mult)
            nc.vector.scalar_tensor_tensor(out=dlt[:, i:i + 1], in0=nm[:, 1, i:i + 1], scalar=nm[:, 0, i:i + 1],
                                           in1=dz[:, i:i + 1], op0=ALU.subtract, op1=ALU.add)

        def exp_sum0(i):
            junk = work.tile([P, V], BF16, name="junk", bufs=2)
            nc.scalar.activation(out=junk[:], in_=nl0[i][:], func=ACT.Exp, scale=-1.0, bias=nm[:, 0, i:i + 1],
                                 accum_out=ssum[:, 0, i:i + 1])

        def exp_sum1(i):
            junk = work.tile([P, V], BF16, name="junk", bufs=2)
            nc.scalar.activation(out=junk[:], in_=l1[i][:], func=ACT.Exp, bias=nm[:, 1, i:i + 1],
                                 accum_out=ssum[:, 1, i:i + 1])

        def exp_diff(i):
            e_t[i] = work.tile([P, V], F32, name="e_t", bufs=LIVE)
            nc.scalar.activation(out=e_t[i][:], in_=dps[i][:], func=ACT.Exp, bias=dlt[:, i:i + 1])

        def clamp(i):
            nc.gpsimd.tensor_scalar(out=e_t[i][:], in0=e_t[i][:], scalar1=RATIO_CAP, scalar2=0.0,
                                    op0=ALU.min, op1=ALU.max)

        def batch_stats(bi, lo, hi):
            n = hi - lo
            zmax = work.tile([P, n], F32, name="zmax", bufs=2)
            zs = work.tile([P, K, n], F32, name="zs", bufs=2)
            ez = work.tile([P, K, n], F32, name="ez", bufs=2)
            sums = work.tile([P, K, n], F32, name="sums", bufs=2)
            ratio = work.tile([P, n], F32, name="ratio", bufs=2)
            rec = work.tile([P, n], F32, name="rec", bufs=2)
            ezs = work.tile([P, n], F32, name="ezs", bufs=2)
            ratio_t[bi] = ratio
            stat_t[bi] = (ezs, sums)
            nc.vector.tensor_max(out=zmax[:], in0=zz[:, 0, lo:hi], in1=zz[:, 1, lo:hi])
            nc.vector.reciprocal(out=rec[:], in_=ssum[:, 1, lo:hi])
            for k in range(K):
                nc.vector.tensor_sub(out=zs[:, k, :], in0=zz[:, k, lo:hi], in1=zmax[:])
            nc.vector.tensor_mul(out=ratio[:], in0=rec[:], in1=ssum[:, 0, lo:hi])
            for k in range(K):
                nc.vector.scalar_tensor_tensor(out=sums[:, k, :], in0=nm[:, k, lo:hi], scalar=math.log(V), in1=zs[:, k, :],
                                               op0=ALU.add, op1=ALU.add)
            nc.scalar.activation(out=ez[:], in_=zs[:], func=ACT.Exp)
            nc.gpsimd.tensor_add(out=ezs[:], in0=ez[:, 0, :], in1=ez[:, 1, :])

        def batch_logs(bi, lo, hi):
            n = hi - lo
            ezs, sums = stat_t[bi]
            lns = work.tile([P, K, n], F32, name="lns", bufs=2)
            lnz = work.tile([P, n], F32, name="lnz", bufs=2)
            bias = work.tile([P, K, n], F32, name="bias", bufs=2)
            bias_t[bi] = bias
            nc.scalar.activation(out=lns[:], in_=ssum[:, :, lo:hi], func=ACT.Ln)
            nc.scalar.activation(out=lnz[:], in_=ezs[:], func=ACT.Ln)
            for k in range(K):
                nc.gpsimd.tensor_add(out=lns[:, k, :], in0=lns[:, k, :], in1=lnz[:])
            for k in range(K):
                nc.gpsimd.tensor_sub(out=bias[:, k, :], in0=sums[:, k, :], in1=lns[:, k, :])

        def log1p(bi, lo, i):
            nc.scalar.activation(out=e_t[i][:], in_=e_t[i][:], func=ACT.Ln,
                                 scale=ratio_t[bi][:, i - lo:i - lo + 1], bias=1.0)

        def finish(bi, lo, i):
            gi, j = divmod(i, TPG)
            w0 = e_t[i]
            nc.vector.scalar_tensor_tensor(out=w0[:], in0=w0[:], scalar=bias_t[bi][:, 0, i - lo:i - lo + 1],
                                           in1=nl0[i][:], op0=ALU.add, op1=ALU.subtract)

        def finish2(bi, lo, i):
            gi, j = divmod(i, TPG)
            o = work.tile([P, V], F32, name="o", bufs=3)
            nc.vector.scalar_tensor_tensor(out=o[:], in0=l1[i][:], scalar=bias_t[bi][:, 1, i - lo:i - lo + 1],
                                           in1=e_t[i][:], op0=ALU.add, op1=ALU.max)
            nc.sync.dma_start(
                out=out[gi * ROWS:(gi + 1) * ROWS, :].rearrange("(r b) v -> r b v", b=TPG)[:, j, :], in_=o[:])

        def prep_w(k):
            wg = work.tile([P, D, 4], BF16, name="wg", bufs=2, align_bytes=64)
            nc.scalar.copy(out=wg[:].rearrange("p (s m) j -> p s m j", s=4),
                           in_=w_raw[k][:].rearrange("p j (m s) -> p s m j", s=4))
            return wg

        def quant_w(k, wg):
            nc.vector.quantize_mx(out=wq[k][:].bitcast(FP8X4), scales=ws[k][:], in_=wg[:].rearrange("p c j -> p (c j)"))

        def prep_emb():
            eb = work.tile([P, V, 4], BF16, name="eb", bufs=1, align_bytes=64)
            nb = work.tile([P, V, 4], BF16, name="nb", bufs=1, align_bytes=64)
            for half in (0, 1):
                pt = psum.tile([P, 2, 256], F32, name="trp", tag="tr", bufs=1)
                transposes(pt, emb_sb[:].bitcast(F32), half)
                nc.vector.tensor_copy(
                    out=eb[:].rearrange("p v t -> p (v t)").bitcast(F32)[:, half * 512:(half + 1) * 512].rearrange("p (v u) -> p v u", u=2),
                    in_=pt[:].rearrange("p u v -> p v u"))
            flat = eb[:].rearrange("p v t -> p (v t)")
            nflat = nb[:].rearrange("p v t -> p (v t)")
            nc.vector.tensor_scalar(out=nflat, in0=flat, scalar1=-1.0, scalar2=None, op0=ALU.mult)
            nc.vector.quantize_mx(out=eq[:].bitcast(FP8X4), scales=es[:], in_=flat)
            nc.vector.quantize_mx(out=neq[:].bitcast(FP8X4), scales=nes[:], in_=nflat)

        def at(step, off):
            q, r = divmod(step - off, TPG)
            return q if r == 0 and 0 <= q < GROUPS else None

        batches = []
        lo = 0
        for hi in BATCH_ENDS:
            batches.append((lo, hi))
            lo = hi

        def c_events(st):
            return [(gi, q // 4, q % 4) for q in range(8) for gi in [at(st, -7 + q // 2)] if gi is not None]

        first = -14
        for step in range(first, TILES + 4):
            i = step
            for gi in range(2, GROUPS):
                if max(4 * gi - 18, first + 1) == step:
                    load(gi)
            if step == first:
                widen(0)
                wg0 = prep_w(0)
                wg1 = prep_w(1)
            if step == first + 3:
                quant_w(0, wg0)
                quant_w(1, wg1)
                nc.vector.tensor_copy(out=g_sb[:], in_=g_raw[:])
                nc.vector.tensor_copy(out=u_sb[:], in_=u_raw[:])
            if step == first + 6:
                prep_emb()

            def tile_at(lag):
                return i - lag if 0 <= i - lag < TILES else None

            cs, nxt = c_events(step), c_events(step + 1)
            gi = at(step, -1)
            if gi is not None:
                z_out(gi)
            if tile_at(1) is not None:
                row_shift(i - 1)
            if tile_at(0) is not None:
                copymax0(i)
                copymax1(i)
            gi = at(step, -1)
            if gi is not None:
                a_quant(gi, 1)
            gi = at(step, -9)
            if gi is not None:
                h_quant(gi)
            for half in (0, 1):
                gi = at(step, -11 + half)
                if gi is not None:
                    h_scale_mul(gi, half)
            gi = at(step, -2)
            if gi is not None:
                a_quant(gi, 0)
            gi = at(step, -4)
            if gi is not None:
                gain(gi, 0)
            for bi, (lo, hi) in enumerate(batches):
                if step == hi + 3:
                    batch_logs(bi, lo, hi)
                    for t in range(lo, hi):
                        log1p(bi, lo, t)
            if cs:
                tanh(*cs[0])
            if tile_at(2) is not None:
                exp_diff(i - 2)
            if tile_at(1) is not None:
                exp_sum0(i - 1)
                exp_sum1(i - 1)
            if len(cs) > 1:
                tanh(*cs[1])
            if tile_at(2) is not None:
                clamp(i - 2)
            gi = at(step, -3)
            if gi is not None:
                gain(gi, 1)
            gi = at(step, -14)
            if gi is not None and gi > 0:
                widen(gi)
            for bi, (lo, hi) in enumerate(batches):
                if step == hi + 2:
                    batch_stats(bi, lo, hi)
            if nxt:
                c_mm(*nxt[0])
            for half in (0, 1):
                gi = at(step, -12 + half)
                if gi is not None:
                    h_transpose(gi, half)
            for k in (0, 1):
                for jj in (0, 1):
                    gi = at(step, -5 + 2 * k + jj)
                    if gi is not None:
                        z_mm(gi, k, 2 * jj)
                        z_mm(gi, k, 2 * jj + 1)
            if len(nxt) > 1:
                c_mm(*nxt[1])
            if tile_at(1) is not None:
                d_mm(i - 1)
            if 0 <= i + 1 < TILES:
                l_mm(i + 1)
            for bi, (lo, hi) in enumerate(batches):
                if step == hi + 3:
                    for t in range(lo, hi):
                        finish(bi, lo, t)
                        if t > lo:
                            finish2(bi, lo, t - 1)
                    finish2(bi, lo, hi - 1)
